import numpy as np
import ml_dtypes


def mxq(x, axis, fmt="e4m3"):
    dtype, down = {"e4m3": (ml_dtypes.float8_e4m3fn, 7), "e5m2": (ml_dtypes.float8_e5m2, 14)}[fmt]
    v = np.moveaxis(np.asarray(x, np.float32).astype(ml_dtypes.bfloat16).astype(np.float64), axis, -1)
    blocks = v.reshape(v.shape[:-1] + (-1, 32))
    amax = np.abs(blocks).max(-1, keepdims=True)
    byte = np.maximum(np.where(amax > 0, np.frexp(amax)[1] - 1 + 127, 0) - down, 1)
    scale = np.exp2(byte - 127.0)
    codes = (blocks / scale).astype(np.float32).astype(dtype).astype(np.float64)
    return np.moveaxis((codes * scale).reshape(v.shape), -1, axis)


WIDE = False


def mx_kscale(k):
    if not WIDE:
        return np.ones(k)
    levels = np.array([10, -10, 5, -5, 0])
    if k % 512:
        return np.exp2(np.random.permutation(np.resize(levels, k // 32))).repeat(32)
    a = np.empty((k // 512, 16))
    for p in range(k // 512):
        a[p, :8] = np.random.permutation(np.resize(levels, 8))
        for g in range(8):
            far = levels[np.abs(levels - a[p, g]) >= 10]
            a[p, g + 8] = far[np.random.randint(len(far))]
    return np.exp2(a.ravel()).repeat(32)


BF16 = ml_dtypes.bfloat16


def bf(x):
    return np.asarray(x, np.float32).astype(BF16)


def f64(x):
    return np.asarray(x).astype(np.float64)


E2M1 = np.array([0.0, 0.5, 1.0, 1.5, 2.0, 3.0, 4.0, 6.0, -0.0, -0.5, -1.0, -1.5, -2.0, -3.0, -4.0, -6.0])


def pack_weight(w, fmt):
    k, n = w.shape
    w = f64(bf(w)).reshape(k // 32, 32, n)
    amax = np.abs(w).max(1)
    if fmt == "e4m3":
        byte = np.frexp(amax)[1] - 1 + 127 - 7
    else:
        mant, ex = np.frexp(amax / 6.0)
        byte = np.where(mant > 0.5, ex, ex - 1) + 127
    byte = np.clip(np.where(amax > 0, byte, 1), 1, 254)
    scaled = (w * np.exp2(127.0 - byte)[:, None, :]).reshape(k, n).astype(np.float32)
    by_word = np.ascontiguousarray(scaled.reshape(k // 512, 128, 4, n).transpose(0, 1, 3, 2))
    if fmt == "e4m3":
        words = by_word.astype(ml_dtypes.float8_e4m3fn).view(np.uint8)
    else:
        c = by_word.astype(ml_dtypes.float4_e2m1fn).view(np.uint8) & 0xF
        words = c[..., 0::2] | (c[..., 1::2] << 4)
    return np.ascontiguousarray(words), np.ascontiguousarray(byte.astype(np.uint8).reshape(k // 512, 16, n))


def unpack_weight(words, scales, fmt):
    g, p, n, _ = words.shape
    if fmt == "e4m3":
        vals = np.ascontiguousarray(words).view(ml_dtypes.float8_e4m3fn).astype(np.float64)
    else:
        nib = np.empty((g, p, n, 4), np.uint8)
        nib[..., 0::2] = words & 0xF
        nib[..., 1::2] = words >> 4
        vals = E2M1[nib]
    vals = vals * np.repeat(np.exp2(scales.astype(np.float64) - 127.0), 8, axis=1)[..., None]
    return vals.transpose(0, 1, 3, 2).reshape(g * 512, n)
def pack4(w):
    words, scales = pack_weight(w, "e2m1")
    return words.reshape(words.shape[0], 128, -1), scales


def unpack4(words, scales):
    return unpack_weight(words.reshape(words.shape[0], 128, -1, 2), scales, "e2m1")


PROBES, PARAMS, REPS = 1024, 2048, 512

OFF_DIAGONAL = 4.0
STEP_SPREAD = 0.2


def setup_inputs():
    u, t = mx_kscale(PARAMS), mx_kscale(PROBES)
    signs = np.where(np.random.standard_normal((PROBES, PARAMS)) > 0, 1.0, -1.0)
    steps = np.exp(STEP_SPREAD * np.random.standard_normal(PARAMS))
    b = np.random.standard_normal((PARAMS, PARAMS))
    h = OFF_DIAGONAL * (b + b.T) / np.sqrt(2 * PARAMS)
    h = h + np.diag(0.5 + np.abs(np.random.standard_normal(PARAMS)))
    avg = np.random.exponential(1.0, (PROBES, REPS)) / PROBES
    avg_words, avg_scales = pack4(avg / t[:, None])
    return {"z": bf(signs * steps * u),
            "h": bf(h / u[:, None] / u),
            "r": bf((1 + 0.1 * np.random.standard_normal(PROBES)) * t),
            "avg_words": avg_words,
            "avg_scales": avg_scales}


def reference(z, h, r, avg_words, avg_scales):
    hz = mxq(f64(z), 1, "e4m3") @ mxq(f64(h), 0, "e4m3")
    e = f64(z) * hz * f64(r)[:, None]
    a = unpack4(avg_words, avg_scales)
    return mxq(e, 0, "e4m3").T @ a

@@ -1,0 +1,293 @@
+from contextlib import ExitStack
+
+import concourse.mybir as mybir
+from concourse.masks import make_identity
+
+PROBES, PARAMS, REPS = 1024, 2048, 512
+FLOPS = 2 * PROBES * PARAMS * PARAMS + 2 * PARAMS * PROBES * REPS
+
+F32 = mybir.dt.float32
+BF16 = mybir.dt.bfloat16
+I32 = mybir.dt.int32
+U32 = mybir.dt.uint32
+U8 = mybir.dt.uint8
+FP8X4 = mybir.dt.float8_e4m3fn_x4
+FP4X4 = mybir.dt.float4_e2m1fn_x4
+MULT = mybir.AluOpType.mult
+
+P = 128
+PACK = 4
+K_PASS = P * PACK
+CHUNK = 512
+RUN = 4
+
+
+def tile_bootstrap_hutchinson_diagonal_s13_kernel(tc, z, h, r, avg_words, avg_scales, out):
+    nc = tc.nc
+    with ExitStack() as ctx:
+        keep = ctx.enter_context(tc.tile_pool(name="keep", bufs=1))
+        rows = ctx.enter_context(tc.tile_pool(name="rows", bufs=16))
+        grouped = ctx.enter_context(tc.tile_pool(name="grouped", bufs=6))
+        results = ctx.enter_context(tc.tile_pool(name="results", bufs=6))
+        psum = ctx.enter_context(tc.psum_pool(name="psum", bufs=1))
+        ctx.enter_context(tc.manual_schedule())
+
+        ident = keep.tile([P, P], F32, name="ident")
+        make_identity(nc, ident[:])
+        r_raw = keep.tile([P, 2, PACK], BF16, name="r_raw")
+        nc.scalar.dma_start(out=r_raw[:], in_=r.rearrange("(q p t) -> p q t", p=P, t=PACK))
+        a_scales = keep.tile([P, 2, REPS], U8, name="a_scales", align_bytes=64)
+        nc.gpsimd.memset(a_scales[:].rearrange("p q n -> p (q n)").bitcast(I32), 0)
+
+        z_rows = z.rearrange("(q p t) k -> q t p k", p=P, t=PACK)
+        z_sb, h_raw = {}, {}
+        a_words = keep.tile([P, 2, 2 * REPS], U8, name="a_words", align_bytes=64)
+
+        def load_z(n):
+            z_sb[n] = keep.tile([P, PARAMS], BF16, name="z%d" % n)
+            nc.sync.dma_start(out=z_sb[n][:], in_=z_rows[n // PACK, n % PACK])
+
+        def load_h(c, g):
+            h_raw[c, g] = rows.tile([P, PACK, CHUNK], BF16, name="h%d%d" % (c, g), tag="rows")
+            block = h[K_PASS * g : K_PASS * (g + 1), CHUNK * c : CHUNK * (c + 1)]
+            nc.sync.dma_start(out=h_raw[c, g][:], in_=block.rearrange("(p t) j -> p t j", t=PACK))
+
+        for k in range(4):
+            load_z(2 * k)
+            load_z(2 * k + 1)
+            load_h(0, k)
+        for c in (1, 2, 3):
+            for g in range(4):
+                load_h(c, g)
+        nc.sync.dma_start(out=a_words[:].bitcast(I32), in_=avg_words.rearrange("q p n -> p q n").bitcast(I32))
+        for quad in range(4):
+            nc.sync.dma_start(
+                out=a_scales[32 * quad : 32 * quad + 4, :, :].bitcast(I32),
+                in_=avg_scales[:, 4 * quad : 4 * quad + 4, :].rearrange("q s n -> s q n").bitcast(I32),
+            )
+
+
+        r_sb = keep.tile([P, 2 * PACK], F32, name="r_sb")
+        free_banks = list(range(8))
+
+        def take_bank():
+            b = free_banks.pop(0)
+            return b, psum.tile([P, CHUNK], F32, name="bank%d" % b, tag="bank%d" % b)
+
+        def copy(engine, dst, src):
+            if engine == "V":
+                nc.vector.tensor_copy(out=dst, in_=src)
+            else:
+                nc.scalar.copy(out=dst, in_=src)
+
+        def quantize(name, src, width):
+            codes = keep.tile([P, width], U32, name="codes_" + name, align_bytes=64)
+            scales = keep.tile([P, width], U8, name="scales_" + name, align_bytes=64)
+            nc.vector.quantize_mx(out=codes[:].bitcast(FP8X4), scales=scales[:], in_=src[:])
+            return codes, scales
+
+        def interleave(engine, src, width):
+            dst = grouped.tile([P, PACK * width], BF16, name="grouped", tag="grouped", align_bytes=64)
+            copy(
+                engine,
+                dst[:].rearrange("p (c i t) -> p c t i", i=RUN, t=PACK),
+                src[:].rearrange("p t (c i) -> p c t i", i=RUN),
+            )
+            return dst
+
+        z_grouped, z_mx, h_grouped, h_mx = {}, {}, {}, {}
+        group, e_rows, e_grouped, e_mx = {}, {}, {}, {}
+
+        def prep_z(n):
+            words = z_sb[n][:].bitcast(F32)
+            z_grouped[n] = grouped.tile([P, PARAMS], BF16, name="grouped", tag="grouped", align_bytes=64)
+            for half in range(2):
+                b, bank = take_bank()
+                for gl in range(2):
+                    g = 2 * half + gl
+                    for u in range(2):
+                        col = (2 * gl + u) * P
+                        nc.tensor.transpose(bank[:, col : col + P], words[:, 256 * g + u : 256 * (g + 1) : 2], ident[:])
+                dst = z_grouped[n][:].bitcast(F32)[:, 512 * half : 512 * (half + 1)]
+                nc.scalar.copy(
+                    out=dst.rearrange("p (g m u) -> p g m u", g=2, u=2),
+                    in_=bank[:].rearrange("p (g u m) -> p g m u", g=2, u=2),
+                )
+                free_banks.append(b)
+
+        def zq(n):
+            z_mx[n] = quantize("z%d" % n, z_grouped[n], 512)
+
+        def hi(c, g, engine):
+            h_grouped[c, g] = interleave(engine, h_raw[c, g], CHUNK)
+
+        def hq(c, g):
+            h_mx[c, g] = quantize("h%d%d" % (c, g), h_grouped[c, g], CHUNK)
+
+        def mm(c, n, g, lo=0, width=CHUNK):
+            if g == 0:
+                group[c, n, lo] = take_bank()
+            bank = group[c, n, lo][1]
+            z_codes, z_scales = z_mx[n]
+            h_codes, h_scales = h_mx[c, g]
+            nc.tensor.matmul_mx(
+                out=bank[:, :width],
+                lhsT=z_codes[:, P * g : P * (g + 1)].bitcast(FP8X4),
+                lhsT_scale=z_scales[:, P * g : P * (g + 1)],
+                rhs=h_codes[:, lo : lo + width].bitcast(FP8X4),
+                rhs_scale=h_scales[:, lo : lo + width],
+                start=(g == 0),
+                stop=(g == 3),
+            )
+
+        def stt(c, n, lo=0, width=CHUNK):
+            q, t = divmod(n, PACK)
+            if t == 0:
+                e_rows[c, q, lo] = rows.tile([P, PACK, width], BF16, name="e_rows", tag="rows")
+            b, bank = group[c, n, lo]
+            j0 = CHUNK * c + lo
+            nc.vector.scalar_tensor_tensor(
+                out=e_rows[c, q, lo][:, t, :],
+                in0=z_sb[n][:, j0 : j0 + width],
+                scalar=r_sb[:, n : n + 1],
+                in1=bank[:, :width],
+                op0=MULT,
+                op1=MULT,
+            )
+            free_banks.append(b)
+
+        def ei(c, q, engine, lo=0, width=CHUNK):
+            e_grouped[c, q, lo] = interleave(engine, e_rows[c, q, lo], width)
+
+        def eq(c, q, lo=0, width=CHUNK):
+            codes, scales = quantize("e%d%d_%d" % (c, q, lo), e_grouped[c, q, lo], width)
+            for j in range(width // P):
+                e_mx[c, q, lo // P + j] = (codes[:, P * j : P * (j + 1)], scales[:, P * j : P * (j + 1)])
+
+        def s2(c, j, engine="S"):
+            b, bank = take_bank()
+            for q in range(2):
+                codes, scales = e_mx[c, q, j]
+                nc.tensor.matmul_mx(
+                    out=bank[:],
+                    lhsT=codes.bitcast(FP8X4),
+                    lhsT_scale=scales,
+                    rhs=a_words[:, q, :].bitcast(FP4X4),
+                    rhs_scale=a_scales[:, q, :],
+                    start=(q == 0),
+                    stop=(q == 1),
+                )
+            result = results.tile([P, REPS], F32, name="result", tag="result")
+            copy(engine, result[:], bank[:])
+            row = CHUNK * c + P * j
+            nc.sync.dma_start(out=out[row : row + P, :], in_=result[:])
+            free_banks.append(b)
+
+        for k in range(4):
+            prep_z(2 * k)
+            prep_z(2 * k + 1)
+            if k > 0:
+                for n in (2 * k - 2, 2 * k - 1):
+                    for g in range(k - 1):
+                        mm(0, n, g)
+                for n in range(2 * k):
+                    mm(0, n, k - 1)
+            zq(2 * k)
+            hi(0, k, "V")
+            zq(2 * k + 1)
+            hq(0, k)
+        nc.vector.tensor_copy(out=r_sb[:], in_=r_raw[:].rearrange("p q t -> p (q t)"))
+        for n in (6, 7):
+            for g in range(3):
+                mm(0, n, g)
+        hi(1, 0, "S")
+        hi(1, 1, "V")
+        hi(1, 2, "S")
+        hq(1, 0)
+        hq(1, 1)
+        hi(1, 3, "S")
+        for n in range(8):
+            mm(0, n, 3)
+        for n in range(8):
+            if n == 4:
+                hq(1, 2)
+            if n == 6:
+                hq(1, 3)
+            stt(0, n)
+
+        def first_half(c):
+            for g in range(4):
+                for n in range(4):
+                    mm(c, n, g)
+
+        for c in (1, 2):
+            first_half(c)
+            if c == 1:
+                hi(2, 0, "S")
+            hq(c + 1, 0)
+            for n in range(4):
+                stt(c, n)
+            for n in range(4, 8):
+                for g in range(4):
+                    mm(c, n, g)
+                if n in (4, 6):
+                    hi(c + 1, n // 2 - 1, "S")
+                    hq(c + 1, n // 2 - 1)
+                stt(c, n)
+            hi(c + 1, 3, "S")
+            if c == 1:
+                hi(3, 0, "V")
+            hq(c + 1, 3)
+        ei(0, 0, "S")
+        ei(1, 0, "S")
+        ei(0, 1, "V")
+        first_half(3)
+        eq(0, 1)
+        eq(0, 0)
+        stt(3, 0)
+        stt(3, 1)
+        ei(1, 1, "V")
+        stt(3, 2)
+        eq(1, 1)
+        stt(3, 3)
+        eq(1, 0)
+        for j in range(4):
+            s2(0, j)
+
+        def piece(lo, width):
+            for n in range(4, 8):
+                for g in range(4):
+                    mm(3, n, g, lo, width)
+
+        def piece_out(lo, width):
+            for n in range(4, 8):
+                stt(3, n, lo, width)
+
+        ei(2, 0, "S")
+        piece(0, 256)
+        ei(2, 1, "V")
+        for j in range(4):
+            s2(1, j)
+        ei(3, 0, "S")
+        piece_out(0, 256)
+        eq(2, 1)
+        eq(2, 0)
+        piece(256, 128)
+        ei(3, 1, "V", 0, 256)
+        for j in range(2):
+            s2(2, j, "V")
+        piece_out(256, 128)
+        piece(384, 128)
+        for j in range(2, 4):
+            s2(2, j)
+        eq(3, 1, 0, 256)
+        ei(3, 1, "V", 256, 128)
+        eq(3, 0)
+        piece_out(384, 128)
+        s2(3, 0)
+        s2(3, 1)
+        eq(3, 1, 256, 128)
+        ei(3, 1, "V", 384, 128)
+        s2(3, 2)
+        eq(3, 1, 384, 128)
+        s2(3, 3, "V")

@@ -86,13 +86,15 @@ def tile_bootstrap_hutchinson_diagonal_s13_kernel(tc, z, h, r, avg_words, avg_sc
             nc.vector.quantize_mx(out=codes[:].bitcast(FP8X4), scales=scales[:], in_=src[:])
             return codes, scales
 
-        def interleave(engine, src, width):
+        def interleave(engines, src, width):
             dst = grouped.tile([P, PACK * width], BF16, name="grouped", tag="grouped", align_bytes=64)
-            copy(
-                engine,
-                dst[:].rearrange("p (c i t) -> p c t i", i=RUN, t=PACK),
-                src[:].rearrange("p t (c i) -> p c t i", i=RUN),
-            )
+            share = width // len(engines)
+            for i, engine in enumerate(engines):
+                copy(
+                    engine,
+                    dst[:, PACK * share * i : PACK * share * (i + 1)].rearrange("p (c i t) -> p c t i", i=RUN, t=PACK),
+                    src[:, :, share * i : share * (i + 1)].rearrange("p t (c i) -> p c t i", i=RUN),
+                )
             return dst
 
         z_grouped, z_mx, h_grouped, h_mx = {}, {}, {}, {}
@@ -220,40 +222,6 @@ def tile_bootstrap_hutchinson_diagonal_s13_kernel(tc, z, h, r, avg_words, avg_sc
                 for n in range(4):
                     mm(c, n, g)
 
-        for c in (1, 2):
-            first_half(c)
-            if c == 1:
-                hi(2, 0, "S")
-            hq(c + 1, 0)
-            for n in range(4):
-                stt(c, n)
-            for n in range(4, 8):
-                for g in range(4):
-                    mm(c, n, g)
-                if n in (4, 6):
-                    hi(c + 1, n // 2 - 1, "S")
-                    hq(c + 1, n // 2 - 1)
-                stt(c, n)
-            hi(c + 1, 3, "S")
-            if c == 1:
-                hi(3, 0, "V")
-            hq(c + 1, 3)
-        ei(0, 0, "S")
-        ei(1, 0, "S")
-        ei(0, 1, "V")
-        first_half(3)
-        eq(0, 1)
-        eq(0, 0)
-        stt(3, 0)
-        stt(3, 1)
-        ei(1, 1, "V")
-        stt(3, 2)
-        eq(1, 1)
-        stt(3, 3)
-        eq(1, 0)
-        for j in range(4):
-            s2(0, j)
-
         def piece(lo, width):
             for n in range(4, 8):
                 for g in range(4):
@@ -263,6 +231,47 @@ def tile_bootstrap_hutchinson_diagonal_s13_kernel(tc, z, h, r, avg_words, avg_sc
             for n in range(4, 8):
                 stt(3, n, lo, width)
 
+        first_half(1)
+        hi(2, 0, "S")
+        hi(2, 1, "VS")
+        hq(2, 0)
+        for n in range(4):
+            stt(1, n)
+        for n in range(4, 8):
+            for g in range(4):
+                mm(1, n, g)
+            if n == 4:
+                hq(2, 1)
+            if n >= 6:
+                hi(2, n - 4, "S")
+                hq(2, n - 4)
+            stt(1, n)
+        hi(3, 0, "V")
+        first_half(2)
+        for n in range(4):
+            stt(2, n)
+        for n in range(4, 8):
+            for g in range(4):
+                mm(2, n, g)
+            if n > 4:
+                hi(3, n - 4, "S")
+            stt(2, n)
+            hq(3, n - 4)
+        ei(0, 0, "S")
+        ei(1, 0, "S")
+        ei(0, 1, "V")
+        first_half(3)
+        eq(0, 0)
+        eq(0, 1)
+        stt(3, 0)
+        stt(3, 1)
+        ei(1, 1, "V")
+        stt(3, 2)
+        eq(1, 1)
+        stt(3, 3)
+        eq(1, 0)
+        for j in range(4):
+            s2(0, j)
         ei(2, 0, "S")
         piece(0, 256)
         ei(2, 1, "V")
@@ -272,22 +281,16 @@ def tile_bootstrap_hutchinson_diagonal_s13_kernel(tc, z, h, r, avg_words, avg_sc
         piece_out(0, 256)
         eq(2, 1)
         eq(2, 0)
-        piece(256, 128)
+        piece(256, 256)
         ei(3, 1, "V", 0, 256)
-        for j in range(2):
-            s2(2, j, "V")
-        piece_out(256, 128)
-        piece(384, 128)
-        for j in range(2, 4):
+        piece_out(256, 256)
+        for j in range(4):
             s2(2, j)
         eq(3, 1, 0, 256)
-        ei(3, 1, "V", 256, 128)
+        ei(3, 1, "V", 256, 256)
         eq(3, 0)
-        piece_out(384, 128)
+        eq(3, 1, 256, 256)
         s2(3, 0)
-        s2(3, 1)
-        eq(3, 1, 256, 128)
-        ei(3, 1, "V", 384, 128)
+        s2(3, 1, "V")
         s2(3, 2)
-        eq(3, 1, 384, 128)
         s2(3, 3, "V")

from contextlib import ExitStack

import concourse.mybir as mybir
from concourse.masks import make_identity

PROBES, PARAMS, REPS = 1024, 2048, 512
FLOPS = 2 * PROBES * PARAMS * PARAMS + 2 * PARAMS * PROBES * REPS

F32 = mybir.dt.float32
BF16 = mybir.dt.bfloat16
I32 = mybir.dt.int32
U32 = mybir.dt.uint32
U8 = mybir.dt.uint8
FP8X4 = mybir.dt.float8_e4m3fn_x4
FP4X4 = mybir.dt.float4_e2m1fn_x4
MULT = mybir.AluOpType.mult

P = 128
PACK = 4
K_PASS = P * PACK
CHUNK = 512
RUN = 4


def tile_bootstrap_hutchinson_diagonal_s13_kernel(tc, z, h, r, avg_words, avg_scales, out):
    nc = tc.nc
    with ExitStack() as ctx:
        keep = ctx.enter_context(tc.tile_pool(name="keep", bufs=1))
        rows = ctx.enter_context(tc.tile_pool(name="rows", bufs=16))
        grouped = ctx.enter_context(tc.tile_pool(name="grouped", bufs=6))
        results = ctx.enter_context(tc.tile_pool(name="results", bufs=6))
        psum = ctx.enter_context(tc.psum_pool(name="psum", bufs=1))
        ctx.enter_context(tc.manual_schedule())

        ident = keep.tile([P, P], F32, name="ident")
        make_identity(nc, ident[:])
        r_raw = keep.tile([P, 2, PACK], BF16, name="r_raw")
        nc.scalar.dma_start(out=r_raw[:], in_=r.rearrange("(q p t) -> p q t", p=P, t=PACK))
        a_scales = keep.tile([P, 2, REPS], U8, name="a_scales", align_bytes=64)
        nc.gpsimd.memset(a_scales[:].rearrange("p q n -> p (q n)").bitcast(I32), 0)

        z_rows = z.rearrange("(q p t) k -> q t p k", p=P, t=PACK)
        z_sb, h_raw = {}, {}
        a_words = keep.tile([P, 2, 2 * REPS], U8, name="a_words", align_bytes=64)

        def load_z(n):
            z_sb[n] = keep.tile([P, PARAMS], BF16, name="z%d" % n)
            nc.sync.dma_start(out=z_sb[n][:], in_=z_rows[n // PACK, n % PACK])

        def load_h(c, g):
            h_raw[c, g] = rows.tile([P, PACK, CHUNK], BF16, name="h%d%d" % (c, g), tag="rows")
            block = h[K_PASS * g : K_PASS * (g + 1), CHUNK * c : CHUNK * (c + 1)]
            nc.sync.dma_start(out=h_raw[c, g][:], in_=block.rearrange("(p t) j -> p t j", t=PACK))

        for k in range(4):
            load_z(2 * k)
            load_z(2 * k + 1)
            load_h(0, k)
        for c in (1, 2, 3):
            for g in range(4):
                load_h(c, g)
        nc.sync.dma_start(out=a_words[:].bitcast(I32), in_=avg_words.rearrange("q p n -> p q n").bitcast(I32))
        for quad in range(4):
            nc.sync.dma_start(
                out=a_scales[32 * quad : 32 * quad + 4, :, :].bitcast(I32),
                in_=avg_scales[:, 4 * quad : 4 * quad + 4, :].rearrange("q s n -> s q n").bitcast(I32),
            )


        r_sb = keep.tile([P, 2 * PACK], F32, name="r_sb")
        free_banks = list(range(8))

        def take_bank():
            b = free_banks.pop(0)
            return b, psum.tile([P, CHUNK], F32, name="bank%d" % b, tag="bank%d" % b)

        def copy(engine, dst, src):
            if engine == "V":
                nc.vector.tensor_copy(out=dst, in_=src)
            else:
                nc.scalar.copy(out=dst, in_=src)

        def quantize(name, src, width):
            codes = keep.tile([P, width], U32, name="codes_" + name, align_bytes=64)
            scales = keep.tile([P, width], U8, name="scales_" + name, align_bytes=64)
            nc.vector.quantize_mx(out=codes[:].bitcast(FP8X4), scales=scales[:], in_=src[:])
            return codes, scales

        def interleave(engines, src, width):
            dst = grouped.tile([P, PACK * width], BF16, name="grouped", tag="grouped", align_bytes=64)
            share = width // len(engines)
            for i, engine in enumerate(engines):
                copy(
                    engine,
                    dst[:, PACK * share * i : PACK * share * (i + 1)].rearrange("p (c i t) -> p c t i", i=RUN, t=PACK),
                    src[:, :, share * i : share * (i + 1)].rearrange("p t (c i) -> p c t i", i=RUN),
                )
            return dst

        z_grouped, z_mx, h_grouped, h_mx = {}, {}, {}, {}
        group, e_rows, e_grouped, e_mx = {}, {}, {}, {}

        def prep_z(n):
            words = z_sb[n][:].bitcast(F32)
            z_grouped[n] = grouped.tile([P, PARAMS], BF16, name="grouped", tag="grouped", align_bytes=64)
            for half in range(2):
                b, bank = take_bank()
                for gl in range(2):
                    g = 2 * half + gl
                    for u in range(2):
                        col = (2 * gl + u) * P
                        nc.tensor.transpose(bank[:, col : col + P], words[:, 256 * g + u : 256 * (g + 1) : 2], ident[:])
                dst = z_grouped[n][:].bitcast(F32)[:, 512 * half : 512 * (half + 1)]
                nc.scalar.copy(
                    out=dst.rearrange("p (g m u) -> p g m u", g=2, u=2),
                    in_=bank[:].rearrange("p (g u m) -> p g m u", g=2, u=2),
                )
                free_banks.append(b)

        def zq(n):
            z_mx[n] = quantize("z%d" % n, z_grouped[n], 512)

        def hi(c, g, engine):
            h_grouped[c, g] = interleave(engine, h_raw[c, g], CHUNK)

        def hq(c, g):
            h_mx[c, g] = quantize("h%d%d" % (c, g), h_grouped[c, g], CHUNK)

        def mm(c, n, g, lo=0, width=CHUNK):
            if g == 0:
                group[c, n, lo] = take_bank()
            bank = group[c, n, lo][1]
            z_codes, z_scales = z_mx[n]
            h_codes, h_scales = h_mx[c, g]
            nc.tensor.matmul_mx(
                out=bank[:, :width],
                lhsT=z_codes[:, P * g : P * (g + 1)].bitcast(FP8X4),
                lhsT_scale=z_scales[:, P * g : P * (g + 1)],
                rhs=h_codes[:, lo : lo + width].bitcast(FP8X4),
                rhs_scale=h_scales[:, lo : lo + width],
                start=(g == 0),
                stop=(g == 3),
            )

        def stt(c, n, lo=0, width=CHUNK):
            q, t = divmod(n, PACK)
            if t == 0:
                e_rows[c, q, lo] = rows.tile([P, PACK, width], BF16, name="e_rows", tag="rows")
            b, bank = group[c, n, lo]
            j0 = CHUNK * c + lo
            nc.vector.scalar_tensor_tensor(
                out=e_rows[c, q, lo][:, t, :],
                in0=z_sb[n][:, j0 : j0 + width],
                scalar=r_sb[:, n : n + 1],
                in1=bank[:, :width],
                op0=MULT,
                op1=MULT,
            )
            free_banks.append(b)

        def ei(c, q, engine, lo=0, width=CHUNK):
            e_grouped[c, q, lo] = interleave(engine, e_rows[c, q, lo], width)

        def eq(c, q, lo=0, width=CHUNK):
            codes, scales = quantize("e%d%d_%d" % (c, q, lo), e_grouped[c, q, lo], width)
            for j in range(width // P):
                e_mx[c, q, lo // P + j] = (codes[:, P * j : P * (j + 1)], scales[:, P * j : P * (j + 1)])

        def s2(c, j, engine="S"):
            b, bank = take_bank()
            for q in range(2):
                codes, scales = e_mx[c, q, j]
                nc.tensor.matmul_mx(
                    out=bank[:],
                    lhsT=codes.bitcast(FP8X4),
                    lhsT_scale=scales,
                    rhs=a_words[:, q, :].bitcast(FP4X4),
                    rhs_scale=a_scales[:, q, :],
                    start=(q == 0),
                    stop=(q == 1),
                )
            result = results.tile([P, REPS], F32, name="result", tag="result")
            copy(engine, result[:], bank[:])
            row = CHUNK * c + P * j
            nc.sync.dma_start(out=out[row : row + P, :], in_=result[:])
            free_banks.append(b)

        for k in range(4):
            prep_z(2 * k)
            prep_z(2 * k + 1)
            if k > 0:
                for n in (2 * k - 2, 2 * k - 1):
                    for g in range(k - 1):
                        mm(0, n, g)
                for n in range(2 * k):
                    mm(0, n, k - 1)
            zq(2 * k)
            hi(0, k, "V")
            zq(2 * k + 1)
            hq(0, k)
        nc.vector.tensor_copy(out=r_sb[:], in_=r_raw[:].rearrange("p q t -> p (q t)"))
        for n in (6, 7):
            for g in range(3):
                mm(0, n, g)
        hi(1, 0, "S")
        hi(1, 1, "V")
        hi(1, 2, "S")
        hq(1, 0)
        hq(1, 1)
        hi(1, 3, "S")
        for n in range(8):
            mm(0, n, 3)
        for n in range(8):
            if n == 4:
                hq(1, 2)
            if n == 6:
                hq(1, 3)
            stt(0, n)

        def first_half(c):
            for g in range(4):
                for n in range(4):
                    mm(c, n, g)

        def piece(lo, width):
            for n in range(4, 8):
                for g in range(4):
                    mm(3, n, g, lo, width)

        def piece_out(lo, width):
            for n in range(4, 8):
                stt(3, n, lo, width)

        first_half(1)
        hi(2, 0, "S")
        hi(2, 1, "VS")
        hq(2, 0)
        for n in range(4):
            stt(1, n)
        for n in range(4, 8):
            for g in range(4):
                mm(1, n, g)
            if n == 4:
                hq(2, 1)
            if n >= 6:
                hi(2, n - 4, "S")
                hq(2, n - 4)
            stt(1, n)
        hi(3, 0, "V")
        first_half(2)
        for n in range(4):
            stt(2, n)
        for n in range(4, 8):
            for g in range(4):
                mm(2, n, g)
            if n > 4:
                hi(3, n - 4, "S")
            stt(2, n)
            hq(3, n - 4)
        ei(0, 0, "S")
        ei(1, 0, "S")
        ei(0, 1, "V")
        first_half(3)
        eq(0, 0)
        eq(0, 1)
        stt(3, 0)
        stt(3, 1)
        ei(1, 1, "V")
        stt(3, 2)
        eq(1, 1)
        stt(3, 3)
        eq(1, 0)
        for j in range(4):
            s2(0, j)
        ei(2, 0, "S")
        piece(0, 256)
        ei(2, 1, "V")
        for j in range(4):
            s2(1, j)
        ei(3, 0, "S")
        piece_out(0, 256)
        eq(2, 1)
        eq(2, 0)
        piece(256, 256)
        ei(3, 1, "V", 0, 256)
        piece_out(256, 256)
        for j in range(4):
            s2(2, j)
        eq(3, 1, 0, 256)
        ei(3, 1, "V", 256, 256)
        eq(3, 0)
        eq(3, 1, 256, 256)
        s2(3, 0)
        s2(3, 1, "V")
        s2(3, 2)
        s2(3, 3, "V")
